import numpy as np
import ml_dtypes

BF16 = ml_dtypes.bfloat16


def bf(x):
    return np.asarray(x, np.float32).astype(BF16)


def f32(x):
    return np.asarray(x, np.float32)


def f64(x):
    return np.asarray(x).astype(np.float64)


def striped(idx):
    return np.concatenate([l.reshape(-1, 16).T for l in idx])


def rows(idx, k):
    return np.tile(np.repeat(idx, 16, axis=0), (k // (16 * 8), 1))


def look(tab, idx):
    return np.take_along_axis(f64(tab), rows(idx, len(tab)), axis=1)


K, S, D, V, N, M = 128, 2048, 2, 1024, 2048, 256


def setup_inputs():
    return {"tab": f32(np.random.standard_normal((K, S))), "th": f32(np.random.standard_normal((K, V))), "w": bf(np.random.standard_normal((K, M)) / np.sqrt(K)), "offs": striped(np.stack([np.random.permutation(S)[:N] for _ in range(8)]))}


def reference(tab, th, w, offs):
    idx = np.stack([g.T.reshape(-1) for g in np.split(offs, 8)])
    x = sum((look(tab, idx[:, d * V:(d + 1) * V]) >= f64(th)) * 1.0 for d in range(D)) / D
    y = f64(w).T @ x
    return y

@@ -1,0 +1,51 @@
+import concourse.mybir as mybir
+
+F32, BF16, U16 = mybir.dt.float32, mybir.dt.bfloat16, mybir.dt.uint16
+ADD, IS_GE = mybir.AluOpType.add, mybir.AluOpType.is_ge
+COPY = mybir.ActivationFunctionType.Copy
+
+K, S = 128, 2048
+D, V = 2, 1024
+M = 256
+N = D * V
+PIECE = 512
+
+FLOPS = 2 * K * M * V + 2 * D * K * V
+
+
+def tile_lookup_vote_ge_none_kernel(tc, tab, th, w, offs, out):
+    nc = tc.nc
+    with (
+        tc.tile_pool(name="held", bufs=1) as held,
+        tc.tile_pool(name="work", bufs=2) as work,
+        tc.psum_pool(name="psum", bufs=4) as psum,
+    ):
+        lists = held.tile([K, N // 16], U16)
+        table = held.tile([K, S], F32)
+        thresholds = held.tile([K, V], F32)
+        weights = held.tile([K, M], BF16)
+        nc.sync.dma_start(lists[:], offs)
+        nc.sync.dma_start(table[:], tab)
+        nc.scalar.dma_start(thresholds[:], th)
+        nc.scalar.dma_start(weights[:], w)
+
+        for j in range(0, V, PIECE):
+            votes = []
+            for ref in range(D):
+                first = (ref * V + j) // 16
+                vote = work.tile([K, PIECE], F32, name=f"vote{ref}")
+                nc.vector.tensor_tensor(
+                    vote[:],
+                    table[:].indirect(lists[:, first : first + PIECE // 16]),
+                    thresholds[:, j : j + PIECE],
+                    IS_GE,
+                )
+                votes.append(vote)
+            count = work.tile([K, PIECE], BF16)
+            nc.vector.tensor_tensor(count[:], votes[0][:], votes[1][:], ADD)
+            for m in range(0, M, 128):
+                product = psum.tile([128, PIECE], F32)
+                nc.tensor.matmul(product[:], weights[:, m : m + 128], count[:], start=True, stop=True)
+                result = work.tile([128, PIECE], F32, name=f"result{m}")
+                nc.scalar.activation(result[:], product[:], COPY, scale=1.0 / D)
+                nc.sync.dma_start(out[m : m + 128, j : j + PIECE], result[:])

@@ -1,7 +1,7 @@
 import concourse.mybir as mybir
 
 F32, BF16, U16 = mybir.dt.float32, mybir.dt.bfloat16, mybir.dt.uint16
-ADD, IS_GE = mybir.AluOpType.add, mybir.AluOpType.is_ge
+IS_GE = mybir.AluOpType.is_ge
 COPY = mybir.ActivationFunctionType.Copy
 
 K, S = 128, 2048
@@ -18,7 +18,7 @@ def tile_lookup_vote_ge_none_kernel(tc, tab, th, w, offs, out):
     with (
         tc.tile_pool(name="held", bufs=1) as held,
         tc.tile_pool(name="work", bufs=2) as work,
-        tc.psum_pool(name="psum", bufs=4) as psum,
+        tc.psum_pool(name="psum", bufs=2) as psum,
     ):
         lists = held.tile([K, N // 16], U16)
         table = held.tile([K, S], F32)
@@ -41,11 +41,14 @@ def tile_lookup_vote_ge_none_kernel(tc, tab, th, w, offs, out):
                     IS_GE,
                 )
                 votes.append(vote)
-            count = work.tile([K, PIECE], BF16)
-            nc.vector.tensor_tensor(count[:], votes[0][:], votes[1][:], ADD)
-            for m in range(0, M, 128):
-                product = psum.tile([128, PIECE], F32)
-                nc.tensor.matmul(product[:], weights[:, m : m + 128], count[:], start=True, stop=True)
+            halves = [vote[:].bitcast(BF16)[:, 1 :: 2] for vote in votes]
+            products = [psum.tile([128, PIECE], F32, name=f"product{m}") for m in range(0, M, 128)]
+            for ref in range(D):
+                for product, m in zip(products, range(0, M, 128)):
+                    nc.tensor.matmul(
+                        product[:], weights[:, m : m + 128], halves[ref], start=ref == 0, stop=ref == D - 1
+                    )
+            for product, m in zip(products, range(0, M, 128)):
                 result = work.tile([128, PIECE], F32, name=f"result{m}")
                 nc.scalar.activation(result[:], product[:], COPY, scale=1.0 / D)
                 nc.sync.dma_start(out[m : m + 128, j : j + PIECE], result[:])

@@ -1,7 +1,7 @@
 import concourse.mybir as mybir
 
 F32, BF16, U16 = mybir.dt.float32, mybir.dt.bfloat16, mybir.dt.uint16
-IS_GE = mybir.AluOpType.is_ge
+IS_GE, MULT = mybir.AluOpType.is_ge, mybir.AluOpType.mult
 COPY = mybir.ActivationFunctionType.Copy
 
 K, S = 128, 2048
@@ -18,16 +18,17 @@ def tile_lookup_vote_ge_none_kernel(tc, tab, th, w, offs, out):
     with (
         tc.tile_pool(name="held", bufs=1) as held,
         tc.tile_pool(name="work", bufs=2) as work,
-        tc.psum_pool(name="psum", bufs=2) as psum,
+        tc.psum_pool(name="psum", bufs=1) as psum,
     ):
         lists = held.tile([K, N // 16], U16)
         table = held.tile([K, S], F32)
-        thresholds = held.tile([K, V], F32)
+        thresholds = [held.tile([K, PIECE], F32, name=f"thresholds{j}") for j in range(0, V, PIECE)]
         weights = held.tile([K, M], BF16)
         nc.sync.dma_start(lists[:], offs)
         nc.sync.dma_start(table[:], tab)
-        nc.scalar.dma_start(thresholds[:], th)
-        nc.scalar.dma_start(weights[:], w)
+        nc.sync.dma_start(thresholds[0][:], th[:, :PIECE])
+        nc.sync.dma_start(weights[:], w)
+        nc.sync.dma_start(thresholds[1][:], th[:, PIECE:])
 
         for j in range(0, V, PIECE):
             votes = []
@@ -37,18 +38,29 @@ def tile_lookup_vote_ge_none_kernel(tc, tab, th, w, offs, out):
                 nc.vector.tensor_tensor(
                     vote[:],
                     table[:].indirect(lists[:, first : first + PIECE // 16]),
-                    thresholds[:, j : j + PIECE],
+                    thresholds[j // PIECE][:],
                     IS_GE,
                 )
                 votes.append(vote)
             halves = [vote[:].bitcast(BF16)[:, 1 :: 2] for vote in votes]
-            products = [psum.tile([128, PIECE], F32, name=f"product{m}") for m in range(0, M, 128)]
+            last = j + PIECE == V
+            width = PIECE // 2 if last else PIECE
+            blocks = [(c, m) for c in range(0, PIECE, width) for m in range(0, M, 128)]
+            products = [psum.tile([128, width], F32, name=f"product_{j + c}_{m}") for c, m in blocks]
             for ref in range(D):
-                for product, m in zip(products, range(0, M, 128)):
+                for product, (c, m) in zip(products, blocks):
                     nc.tensor.matmul(
-                        product[:], weights[:, m : m + 128], halves[ref], start=ref == 0, stop=ref == D - 1
+                        product[:],
+                        weights[:, m : m + 128],
+                        halves[ref][:, c : c + width],
+                        start=ref == 0,
+                        stop=ref == D - 1,
                     )
-            for product, m in zip(products, range(0, M, 128)):
-                result = work.tile([128, PIECE], F32, name=f"result{m}")
-                nc.scalar.activation(result[:], product[:], COPY, scale=1.0 / D)
-                nc.sync.dma_start(out[m : m + 128, j : j + PIECE], result[:])
+            for product, (c, m) in zip(products, blocks):
+                result = work.tile([128, width], F32, name=f"result_{j + c}_{m}")
+                if last and m > 0:
+                    nc.vector.tensor_scalar(result[:], product[:], 1.0 / D, None, MULT)
+                    nc.sync.dma_start(out[m : m + 128, j + c : j + c + width], result[:])
+                else:
+                    nc.scalar.activation(result[:], product[:], COPY, scale=1.0 / D)
+                    nc.scalar.dma_start(out[m : m + 128, j + c : j + c + width], result[:])

import concourse.mybir as mybir

F32, BF16, U16 = mybir.dt.float32, mybir.dt.bfloat16, mybir.dt.uint16
IS_GE, MULT = mybir.AluOpType.is_ge, mybir.AluOpType.mult
COPY = mybir.ActivationFunctionType.Copy

K, S = 128, 2048
D, V = 2, 1024
M = 256
N = D * V
PIECE = 512

FLOPS = 2 * K * M * V + 2 * D * K * V


def tile_lookup_vote_ge_none_kernel(tc, tab, th, w, offs, out):
    nc = tc.nc
    with (
        tc.tile_pool(name="held", bufs=1) as held,
        tc.tile_pool(name="work", bufs=2) as work,
        tc.psum_pool(name="psum", bufs=1) as psum,
    ):
        lists = held.tile([K, N // 16], U16)
        table = held.tile([K, S], F32)
        thresholds = [held.tile([K, PIECE], F32, name=f"thresholds{j}") for j in range(0, V, PIECE)]
        weights = held.tile([K, M], BF16)
        nc.sync.dma_start(lists[:], offs)
        nc.sync.dma_start(table[:], tab)
        nc.sync.dma_start(thresholds[0][:], th[:, :PIECE])
        nc.sync.dma_start(weights[:], w)
        nc.sync.dma_start(thresholds[1][:], th[:, PIECE:])

        for j in range(0, V, PIECE):
            votes = []
            for ref in range(D):
                first = (ref * V + j) // 16
                vote = work.tile([K, PIECE], F32, name=f"vote{ref}")
                nc.vector.tensor_tensor(
                    vote[:],
                    table[:].indirect(lists[:, first : first + PIECE // 16]),
                    thresholds[j // PIECE][:],
                    IS_GE,
                )
                votes.append(vote)
            halves = [vote[:].bitcast(BF16)[:, 1 :: 2] for vote in votes]
            last = j + PIECE == V
            width = PIECE // 2 if last else PIECE
            blocks = [(c, m) for c in range(0, PIECE, width) for m in range(0, M, 128)]
            products = [psum.tile([128, width], F32, name=f"product_{j + c}_{m}") for c, m in blocks]
            for ref in range(D):
                for product, (c, m) in zip(products, blocks):
                    nc.tensor.matmul(
                        product[:],
                        weights[:, m : m + 128],
                        halves[ref][:, c : c + width],
                        start=ref == 0,
                        stop=ref == D - 1,
                    )
            for product, (c, m) in zip(products, blocks):
                result = work.tile([128, width], F32, name=f"result_{j + c}_{m}")
                if last and m > 0:
                    nc.vector.tensor_scalar(result[:], product[:], 1.0 / D, None, MULT)
                    nc.sync.dma_start(out[m : m + 128, j + c : j + c + width], result[:])
                else:
                    nc.scalar.activation(result[:], product[:], COPY, scale=1.0 / D)
                    nc.scalar.dma_start(out[m : m + 128, j + c : j + c + width], result[:])
